import numpy as np
import ml_dtypes


def mxq(x, axis, fmt="e4m3"):
    dtype, down = {"e4m3": (ml_dtypes.float8_e4m3fn, 7), "e5m2": (ml_dtypes.float8_e5m2, 14)}[fmt]
    v = np.moveaxis(np.asarray(x, np.float32).astype(ml_dtypes.bfloat16).astype(np.float64), axis, -1)
    blocks = v.reshape(v.shape[:-1] + (-1, 32))
    amax = np.abs(blocks).max(-1, keepdims=True)
    byte = np.maximum(np.where(amax > 0, np.frexp(amax)[1] - 1 + 127, 0) - down, 1)
    scale = np.exp2(byte - 127.0)
    codes = (blocks / scale).astype(np.float32).astype(dtype).astype(np.float64)
    return np.moveaxis((codes * scale).reshape(v.shape), -1, axis)


WIDE = False


def mx_kscale(k):
    if not WIDE:
        return np.ones(k)
    levels = np.array([10, -10, 5, -5, 0])
    if k % 512:
        return np.exp2(np.random.permutation(np.resize(levels, k // 32))).repeat(32)
    a = np.empty((k // 512, 16))
    for p in range(k // 512):
        a[p, :8] = np.random.permutation(np.resize(levels, 8))
        for g in range(8):
            far = levels[np.abs(levels - a[p, g]) >= 10]
            a[p, g + 8] = far[np.random.randint(len(far))]
    return np.exp2(a.ravel()).repeat(32)


BF16 = ml_dtypes.bfloat16


def bf(x):
    return np.asarray(x, np.float32).astype(BF16)


def f64(x):
    return np.asarray(x).astype(np.float64)


E2M1 = np.array([0.0, 0.5, 1.0, 1.5, 2.0, 3.0, 4.0, 6.0, -0.0, -0.5, -1.0, -1.5, -2.0, -3.0, -4.0, -6.0])


def pack_weight(w, fmt):
    k, n = w.shape
    w = f64(bf(w)).reshape(k // 32, 32, n)
    amax = np.abs(w).max(1)
    if fmt == "e4m3":
        byte = np.frexp(amax)[1] - 1 + 127 - 7
    else:
        mant, ex = np.frexp(amax / 6.0)
        byte = np.where(mant > 0.5, ex, ex - 1) + 127
    byte = np.clip(np.where(amax > 0, byte, 1), 1, 254)
    scaled = (w * np.exp2(127.0 - byte)[:, None, :]).reshape(k, n).astype(np.float32)
    by_word = np.ascontiguousarray(scaled.reshape(k // 512, 128, 4, n).transpose(0, 1, 3, 2))
    if fmt == "e4m3":
        words = by_word.astype(ml_dtypes.float8_e4m3fn).view(np.uint8)
    else:
        c = by_word.astype(ml_dtypes.float4_e2m1fn).view(np.uint8) & 0xF
        words = c[..., 0::2] | (c[..., 1::2] << 4)
    return np.ascontiguousarray(words), np.ascontiguousarray(byte.astype(np.uint8).reshape(k // 512, 16, n))


def unpack_weight(words, scales, fmt):
    g, p, n, _ = words.shape
    if fmt == "e4m3":
        vals = np.ascontiguousarray(words).view(ml_dtypes.float8_e4m3fn).astype(np.float64)
    else:
        nib = np.empty((g, p, n, 4), np.uint8)
        nib[..., 0::2] = words & 0xF
        nib[..., 1::2] = words >> 4
        vals = E2M1[nib]
    vals = vals * np.repeat(np.exp2(scales.astype(np.float64) - 127.0), 8, axis=1)[..., None]
    return vals.transpose(0, 1, 3, 2).reshape(g * 512, n)
def pack4(w):
    words, scales = pack_weight(w, "e2m1")
    return words.reshape(words.shape[0], 128, -1), scales


def unpack4(words, scales):
    return unpack_weight(words.reshape(words.shape[0], 128, -1, 2), scales, "e2m1")


S, G, R, T, N = 1024, 1024, 1024, 2048, 512


def draw0():
    s = mx_kscale(G)
    t = mx_kscale(R)
    u = mx_kscale(S)
    lig = np.random.standard_normal((S, G)) * s * u[:, None]
    inter = np.random.standard_normal((G, R)) / np.sqrt(G) / s[:, None] * t
    rec = np.abs(np.random.standard_normal((R, T))) ** 3 / R / t[:, None]
    rec_words, rec_scales = pack4(rec)
    niche = np.random.standard_normal((N, S)) / np.sqrt(S) / u
    kd = (0.5 + np.random.random(S)) * u
    return {"lig": bf(lig),
            "inter": bf(inter),
            "rec_words": rec_words,
            "rec_scales": rec_scales,
            "niche": bf(niche),
            "kd": bf(kd)}


def core(lig, inter, rec_words, rec_scales, niche, kd):
    rec = unpack4(rec_words, rec_scales)
    d = mxq(f64(lig), 1, "e4m3") @ mxq(f64(inter), 0, "e4m3")
    h = np.maximum(d, 0.0)
    a = mxq(h, 1, "e4m3") @ rec
    score = a / (f64(kd)[:, None] + a)
    contrast = mxq(f64(niche), 1, "e4m3") @ mxq(h, 0, "e4m3")
    return score, contrast


def e4m3fn_bytes(y):
    return np.clip(np.asarray(y, np.float64), -448.0, 448.0).astype(np.float32).astype(ml_dtypes.float8_e4m3fn).view(np.uint8)


def e4m3fn_values(b):
    return np.asarray(b, np.uint8).view(ml_dtypes.float8_e4m3fn).astype(np.float64)


def setup_inputs():
    d = draw0()
    x0 = np.asarray(d['niche']).astype(np.float64)
    s = (np.max(np.abs(x0), axis=(0,), keepdims=True) / 448.0).astype(np.float32)
    out = {}
    for k, v in d.items():
        if k == 'niche':
            out['niche_bytes'] = e4m3fn_bytes(x0 / s.astype(np.float64))
            out['niche_scale'] = s
        else:
            out[k] = v
    return out


def reference(lig, inter, rec_words, rec_scales, niche_bytes, niche_scale, kd):
    return core(lig, inter, rec_words, rec_scales, e4m3fn_values(niche_bytes) * niche_scale.astype(np.float64), kd)

@@ -1,0 +1,304 @@
+from contextlib import ExitStack
+
+import concourse.mybir as mybir
+from concourse.masks import make_identity
+
+S, LIG, R, T, N = 1024, 1024, 1024, 2048, 512
+FLOPS = 2 * (S * LIG * R + S * R * T + N * S * R)
+
+P = 128
+F32 = mybir.dt.float32
+BF16 = mybir.dt.bfloat16
+U32 = mybir.dt.uint32
+I32 = mybir.dt.int32
+U8 = mybir.dt.uint8
+FP8 = mybir.dt.float8_e4m3fn
+FP8X4 = mybir.dt.float8_e4m3fn_x4
+FP4X4 = mybir.dt.float4_e2m1fn_x4
+ACT = mybir.ActivationFunctionType
+ALU = mybir.AluOpType
+
+
+def tile_ligand_receptor_signalling_s8_kernel(
+    tc, lig, inter, rec_words, rec_scales, niche_bytes, niche_scale, kd, score, contrast
+):
+    nc = tc.nc
+    V, SC, TE = nc.vector, nc.scalar, nc.tensor
+
+    with ExitStack() as ctx:
+        keep = ctx.enter_context(tc.tile_pool(name="keep", bufs=1))
+        work = ctx.enter_context(tc.tile_pool(name="work", bufs=3))
+        psum = ctx.enter_context(tc.psum_pool(name="psum", bufs=1))
+        ctx.enter_context(tc.manual_schedule())
+
+        def kt(name, shape, dt):
+            return keep.tile(shape, dt, name=name, align_bytes=64)
+
+        kd_sb = kt("kd_sb", [P, 8], BF16)
+        nsc = kt("nsc", [P, 8], F32)
+        nc.scalar.dma_start(out=kd_sb[:].rearrange("p (g t) -> p g t", g=2), in_=kd.rearrange("(g m t) -> m g t", g=2, t=4))
+        nc.scalar.dma_start(out=nsc[:].rearrange("p (g t) -> p g t", g=2), in_=niche_scale.rearrange("o (g p t) -> p (o g) t", g=2, t=4))
+
+        rec_s = kt("rec_s", [P, 2, T], U8)
+        nc.gpsimd.memset(rec_s[:].rearrange("p g n -> p (g n)").bitcast(I32), 0)
+        ident = kt("ident", [P, P], F32)
+        make_identity(nc, ident[:])
+
+        i_raw = [kt("i_raw%d" % g, [P, 4, R], BF16) for g in range(2)]
+        inter_v = inter.rearrange("(g p j) r -> g p j r", g=2, j=4)
+        l_raw = [kt("l_raw%d" % b, [P, LIG], BF16) for b in range(8)]
+        lig_v = lig.rearrange("(g m t) k -> g m t k", g=2, t=4)
+        rec_w = kt("rec_w", [P, 2, 2 * T], U8)
+        n_raw = kt("n_raw", [P, 4, S], U8)
+
+        def load_lig(b):
+            nc.sync.dma_start(out=l_raw[b][:], in_=lig_v[b // 4, :, b % 4, :])
+
+        def load_i(g):
+            nc.sync.dma_start(out=i_raw[g][:], in_=inter_v[g])
+
+        def load_n():
+            nc.sync.dma_start(out=n_raw[:], in_=niche_bytes.rearrange("(a p) s -> p a s", p=P))
+
+        def load_rs():
+            for q in range(4):
+                nc.sync.dma_start(
+                    out=rec_s[32 * q : 32 * q + 4, :, :].bitcast(I32),
+                    in_=rec_scales[:, 4 * q : 4 * q + 4, :].rearrange("g q n -> q g n").bitcast(I32),
+                )
+
+        def load_rw(g):
+            nc.sync.dma_start(out=rec_w[:, g, :], in_=rec_words[g])
+
+        loads = {"i": load_i, "l": load_lig, "n": load_n, "rs": load_rs, "rw": load_rw}
+        LOADS=[('i',0),('i',1),('l',0),('l',1),('l',2),('l',3),('n',),('rs',),('rw',0),('rw',1),('l',4),('l',5),('l',6),('l',7)]
+        for item in LOADS:
+            loads[item[0]](*item[1:])
+
+        warm = kt("warm", [P, 1], F32)
+        nc.gpsimd.memset(warm[:], 1.0)
+        SC.activation(out=warm[:], in_=warm[:], func=ACT.Abs_reciprocal_sqrt)
+
+        def mx(out, a, asc, b, bsc, start, stop, bdt=FP8X4):
+            TE.matmul_mx(out=out, lhsT=a.bitcast(FP8X4), lhsT_scale=asc, rhs=b.bitcast(bdt), rhs_scale=bsc, start=start, stop=stop)
+
+        def quant(codes, scales, src):
+            V.quantize_mx(out=codes.bitcast(FP8X4), scales=scales, in_=src)
+
+        def copy(eng, out, in_):
+            if eng is SC:
+                SC.copy(out=out, in_=in_)
+            else:
+                V.tensor_copy(out=out, in_=in_)
+
+        i_grp = [[kt("i_grp%d%d" % (g, h), [P, 2, P, 2, 4], BF16) for h in range(2)] for g in range(2)]
+        i_codes = [kt("i_codes%d" % g, [P, R], U32) for g in range(2)]
+        i_scales = [kt("i_scales%d" % g, [P, R], U8) for g in range(2)]
+
+        def inter_piece(g, h, u, eng):
+            src = i_raw[g][:, :, 512 * h : 512 * h + 512].rearrange("p j (q u e) -> p u q e j", u=2, e=2)
+            copy(eng, i_grp[g][h][:, u], src[:, u])
+
+        def inter_quant(g, h):
+            cols = slice(512 * h, 512 * h + 512)
+            quant(i_codes[g][:, cols], i_scales[g][:, cols], i_grp[g][h][:].rearrange("p u q e j -> p (u q e j)"))
+
+        def word_transposes(words, step2):
+            bank = psum.tile([P, 4, P], F32, name="tr", tag="tr", bufs=2)
+            for c in range(4):
+                if step2:
+                    w = words[:, 256 * (c // 2) + c % 2 : 256 * (c // 2 + 1) : 2]
+                else:
+                    w = words[:, 128 * c : 128 * c + 128]
+                TE.transpose(bank[:, c, :], w, ident[:])
+            return bank
+
+        l_grp = [None] * 8
+        l_codes = [kt("l_codes%d" % b, [P, 2 * P], U32) for b in range(8)]
+        l_scales = [kt("l_scales%d" % b, [P, 2 * P], U8) for b in range(8)]
+        bank_of = {}
+
+        def lig_T(b):
+            bank_of["l", b] = word_transposes(l_raw[b][:].bitcast(F32), True)
+
+        def lig_copy(b, eng):
+            l_grp[b] = work.tile([P, 2, P, 4], BF16, name="l_grp", align_bytes=64)
+            dst = l_grp[b][:].rearrange("p g m t -> p (g m t)").bitcast(F32).rearrange("p (g m u) -> p g m u", g=2, u=2)
+            copy(eng, dst, bank_of["l", b][:].rearrange("p (g u) m -> p g m u", u=2))
+
+        def lig_quant(b):
+            quant(l_codes[b][:], l_scales[b][:], l_grp[b][:].rearrange("p g m t -> p (g m t)"))
+
+        H = [kt("H%d" % g, [P, 4, R], BF16) for g in range(2)]
+
+        def h_mm1(b, h):
+                bank = psum.tile([P, 512], F32, name="hb", tag="hb", bufs=3)
+                bank_of["h", b, h] = bank
+                cols = slice(512 * h, 512 * h + 512)
+                for g in range(2):
+                    rows = slice(P * g, P * g + P)
+                    mx(bank[:], l_codes[b][:, rows], l_scales[b][:, rows], i_codes[g][:, cols], i_scales[g][:, cols], g == 0, g == 1)
+
+        def h_relu(b, h, eng):
+            out = H[b // 4][:, b % 4, 512 * h : 512 * h + 512]
+            if eng is SC:
+                SC.activation(out=out, in_=bank_of["h", b, h][:], func=ACT.Relu)
+            else:
+                V.tensor_scalar(out=out, in0=bank_of["h", b, h][:], scalar1=0.0, scalar2=None, op0=ALU.max)
+
+        t_grp = [None] * 8
+        t_codes = [kt("t_codes%d" % b, [P, 2 * P], U32) for b in range(8)]
+        t_scales = [kt("t_scales%d" % b, [P, 2 * P], U8) for b in range(8)]
+
+        def ht_T(b):
+            bank_of["t", b] = word_transposes(H[b // 4][:, b % 4, :].bitcast(F32), False)
+
+        def ht_copy(b, eng):
+            t_grp[b] = work.tile([P, 2, P, 4], BF16, name="t_grp", align_bytes=64)
+            dst = t_grp[b][:].rearrange("p g m t -> p (g m t)").bitcast(F32).rearrange("p (g m u) -> p g m u", g=2, u=2)
+            copy(eng, dst, bank_of["t", b][:].rearrange("p (g u) m -> p g m u", u=2))
+
+        def ht_quant(b):
+            quant(t_codes[b][:], t_scales[b][:], t_grp[b][:].rearrange("p g m t -> p (g m t)"))
+
+        rkd = kt("rkd", [P, 8], F32)
+        q_of = [None] * 8
+
+        def a_mm(b, n):
+            bank = psum.tile([P, 512], F32, name="ab", tag="ab", bufs=3)
+            for g in range(2):
+                rows = slice(P * g, P * g + P)
+                mx(bank[:], t_codes[b][:, rows], t_scales[b][:, rows], rec_w[:, g, 1024 * n : 1024 * n + 1024],
+                   rec_s[:, g, 512 * n : 512 * n + 512], g == 0, g == 1, FP4X4)
+            if n == 0:
+                q_of[b] = work.tile([P, T], F32, name="q", bufs=4, align_bytes=64)
+            SC.activation(out=q_of[b][:, 512 * n : 512 * n + 512], in_=bank[:], func=ACT.Abs_reciprocal_sqrt,
+                          scale=rkd[:, b : b + 1], bias=1.0)
+
+        def hill_square(b, c):
+            cols = slice(512 * c[0], 512 * c[1])
+            SC.activation(out=q_of[b][:, cols], in_=q_of[b][:, cols], func=ACT.Square)
+
+        def hill_out(b, c, eng):
+            cols = slice(512 * c[0], 512 * c[1])
+            eng.tensor_scalar(out=q_of[b][:, cols], in0=q_of[b][:, cols], scalar1=-1.0, scalar2=1.0, op0=ALU.mult, op1=ALU.add)
+            nc.sync.dma_start(out=score.rearrange("(g m t) n -> g t m n", g=2, t=4)[b // 4, b % 4][:, cols], in_=q_of[b][:, cols])
+
+        s_grp = [kt("s_grp%d" % g, [P, R, 4], BF16) for g in range(2)]
+        s_codes = [kt("s_codes%d" % g, [P, R], U32) for g in range(2)]
+        s_scales = [kt("s_scales%d" % g, [P, R], U8) for g in range(2)]
+
+        def hs_piece(g, k, eng):
+            cols = slice(256 * k, 256 * k + 256)
+            copy(eng, s_grp[g][:, cols, :], H[g][:, :, cols].rearrange("p t r -> p r t"))
+
+        def hs_quant(g, h):
+            cols = slice(512 * h, 512 * h + 512)
+            quant(s_codes[g][:, cols], s_scales[g][:, cols], s_grp[g][:, cols, :].rearrange("p r t -> p (r t)"))
+
+        n_bf = [None] * 4
+        n_grp = [None] * 4
+        n_codes = [kt("n_codes%d" % a, [P, 2 * P], U32) for a in range(4)]
+        n_scales = [kt("n_scales%d" % a, [P, 2 * P], U8) for a in range(4)]
+
+        def n_widen(a, eng):
+            n_bf[a] = kt("n_bf%d" % a, [P, S], BF16)
+            copy(eng, n_bf[a][:], n_raw[:, a, :].bitcast(FP8))
+
+        def n_T(a):
+            bank_of["n", a] = word_transposes(n_bf[a][:].bitcast(F32), True)
+
+        def n_scale(a):
+            n_grp[a] = kt("n_grp%d" % a, [P, 2, P, 4], BF16)
+            src = bank_of["n", a][:].rearrange("p c n -> p (c n)").bitcast(BF16).rearrange("p (g u n e) -> p g n u e", g=2, u=2, e=2)
+            for g in range(2):
+                sc = nsc[:, 4 * g : 4 * g + 4].rearrange("p (u e) -> p u e", e=2).unsqueeze(1).to_broadcast([P, P, 2, 2])
+                V.tensor_tensor(out=n_grp[a][:, g].rearrange("p n (u e) -> p n u e", e=2), in0=src[:, g], in1=sc, op=ALU.mult)
+
+        def n_quant(a):
+            quant(n_codes[a][:], n_scales[a][:], n_grp[a][:].rearrange("p g n t -> p (g n t)"))
+
+        c_out = [kt("c_out%d" % a, [P, R], F32) for a in range(4)]
+
+        def c_mm(a, h):
+            bank = psum.tile([P, 512], F32, name="hb", tag="hb", bufs=3)
+            bank_of["c", a, h] = bank
+            cols = slice(512 * h, 512 * h + 512)
+            for g in range(2):
+                rows = slice(P * g, P * g + P)
+                mx(bank[:], n_codes[a][:, rows], n_scales[a][:, rows], s_codes[g][:, cols], s_scales[g][:, cols], g == 0, g == 1)
+
+        def c_copy(a, h, eng):
+            copy(eng, c_out[a][:, 512 * h : 512 * h + 512].rearrange("p (q u e) -> p q u e", u=2, e=2),
+                 bank_of["c", a, h][:].rearrange("p (u q e) -> p q u e", u=2, e=2))
+
+        def c_store(a, h):
+            cols = slice(512 * h, 512 * h + 512)
+            nc.sync.dma_start(out=contrast[P * a : P * a + P, cols], in_=c_out[a][:, cols])
+
+        def recip_kd():
+            V.reciprocal(out=rkd[:], in_=kd_sb[:])
+
+        calls = {
+            "inter_piece": inter_piece, "inter_quant": inter_quant, "lig_T": lig_T, "lig_copy": lig_copy, "lig_quant": lig_quant,
+            "h_mm1": h_mm1, "h_relu": h_relu, "ht_T": ht_T, "ht_copy": ht_copy, "ht_quant": ht_quant, "hs_piece": hs_piece, "hs_quant": hs_quant,
+            "n_widen": n_widen, "n_T": n_T, "n_scale": n_scale, "n_quant": n_quant, "c_mm": c_mm, "c_copy": c_copy, "c_store": c_store,
+        }
+        engines = {"V": V, "S": SC, "G": nc.gpsimd}
+
+        def run(items):
+            for f in items:
+                calls[f[0]](*[engines.get(z, z) for z in f[1:]])
+
+
+        AFF=lambda b,n:'G'
+        RE=lambda b,h:'S' if (b,h) in((2,1),) else 'V'
+        NT={3:0,4:1,5:2,6:3}
+        hs=lambda g,k:('hs_piece',g,k,'V')
+        hq=lambda g,h:('hs_quant',g,h)
+        lc=lambda b:('lig_copy',b,'V'); lq=lambda b:('lig_quant',b)
+        ns=lambda a:('n_scale',a); nq=lambda a:('n_quant',a)
+        FILL={0:[[lc(4)],[],[lq(4)],[],[]],
+         1:[[lc(5)],[lq(5)],[hs(0,0)],[hs(0,1)],[]],
+         2:[[lc(6)],[lq(6)],[hs(0,2)],[hs(0,3)],[hq(0,0)]],
+         3:[[lc(7)],[lq(7)],[hq(0,1)],[],[ns(0)]],
+         4:[[nq(0),ns(1)],[],[],[nq(1)],[]],
+         5:[[ns(2)],[],[nq(2)],[],[]],
+         6:[[hs(1,0)],[hs(1,1),ns(3)],[],[],[nq(3),hs(1,2),hq(1,0),hs(1,3),hq(1,1)]],
+         7:[[],[],[],[],[]]}
+        LAST=[]
+        for a in range(4):
+            for h in range(2): LAST+=[('c_mm',a,h),('c_copy',a,h,'V'),('c_store',a,h)]
+
+
+        lig_T(0); lig_T(1)
+        inter_piece(0,0,0,V); inter_piece(0,0,1,SC); inter_piece(0,1,0,V); inter_piece(0,1,1,SC)
+        inter_quant(0,0); inter_piece(1,0,0,V); inter_piece(1,0,1,SC); inter_quant(0,1); inter_piece(1,1,0,V)
+        recip_kd(); lig_copy(0,SC); inter_quant(1,0); inter_piece(1,1,1,SC); lig_quant(0); lig_copy(1,SC); inter_quant(1,1)
+        h_mm1(0,0); h_relu(0,0,V); h_mm1(0,1); h_relu(0,1,SC); lig_quant(1)
+        n_widen(0,V)
+        h_mm1(1,0); h_relu(1,0,V); h_mm1(1,1);
+        ht_T(0); h_relu(1,1,SC); ht_copy(0,V)
+        lig_T(2); lig_copy(2,SC); n_widen(1,V); ht_quant(0); lig_quant(2); lig_T(3); lig_copy(3,SC); n_widen(2,V);  n_widen(3,V); lig_quant(3)
+        sq=[]
+        fill=FILL
+        for b in range(8):
+            for n in range(4):
+                a_mm(b,n)
+                sq.append((b,n))
+                if len(sq)>1:
+                    x,y=sq.pop(0); hill_square(x,(y,y+1)); hill_out(x,(y,y+1),engines[AFF(x,y)])
+                if n==1:
+                    if b<7: ht_T(b+1)
+                    if b<4: lig_T(b+4)
+                    if b in NT: n_T(NT[b])
+                    if b<7: ht_copy(b+1,V)
+                    run(fill[b][0])
+                    if b<7: ht_quant(b+1)
+                    run(fill[b][1])
+                if n>=2 and b<6:
+                    h_mm1(b+2,n-2); h_relu(b+2,n-2,engines[RE(b+2,n-2)])
+                    run(fill[b][n])
+            run(fill[b][4])
+        x,y=sq.pop(0); hill_square(x,(y,y+1)); hill_out(x,(y,y+1),engines[AFF(x,y)])
+        run(LAST)

@@ -44,9 +44,9 @@ def tile_ligand_receptor_signalling_s8_kernel(
         ident = kt("ident", [P, P], F32)
         make_identity(nc, ident[:])
 
-        i_raw = [kt("i_raw%d" % g, [P, 4, R], BF16) for g in range(2)]
+        i_raw = [work.tile([P, 4, R], BF16, name="raw%d" % g, tag="raw", bufs=2, align_bytes=64) for g in range(2)]
         inter_v = inter.rearrange("(g p j) r -> g p j r", g=2, j=4)
-        l_raw = [kt("l_raw%d" % b, [P, LIG], BF16) for b in range(8)]
+        l_raw = [work.tile([P, LIG], BF16, name="l_raw%d" % b, tag="lraw", bufs=8, align_bytes=64) for b in range(8)]
         lig_v = lig.rearrange("(g m t) k -> g m t k", g=2, t=4)
         rec_w = kt("rec_w", [P, 2, 2 * T], U8)
         n_raw = kt("n_raw", [P, 4, S], U8)
@@ -170,9 +170,12 @@ def tile_ligand_receptor_signalling_s8_kernel(
                 rows = slice(P * g, P * g + P)
                 mx(bank[:], t_codes[b][:, rows], t_scales[b][:, rows], rec_w[:, g, 1024 * n : 1024 * n + 1024],
                    rec_s[:, g, 512 * n : 512 * n + 512], g == 0, g == 1, FP4X4)
-            if n == 0:
-                q_of[b] = work.tile([P, T], F32, name="q", bufs=4, align_bytes=64)
-            SC.activation(out=q_of[b][:, 512 * n : 512 * n + 512], in_=bank[:], func=ACT.Abs_reciprocal_sqrt,
+            bank_of["a", b, n] = bank
+
+        def hill_rsqrt(b, n):
+            if q_of[b] is None:
+                q_of[b] = kt("q%d" % b, [P, T], F32)
+            SC.activation(out=q_of[b][:, 512 * n : 512 * n + 512], in_=bank_of["a", b, n][:], func=ACT.Abs_reciprocal_sqrt,
                           scale=rkd[:, b : b + 1], bias=1.0)
 
         def hill_square(b, c):
@@ -182,9 +185,12 @@ def tile_ligand_receptor_signalling_s8_kernel(
         def hill_out(b, c, eng):
             cols = slice(512 * c[0], 512 * c[1])
             eng.tensor_scalar(out=q_of[b][:, cols], in0=q_of[b][:, cols], scalar1=-1.0, scalar2=1.0, op0=ALU.mult, op1=ALU.add)
+
+        def hill_store(b, c):
+            cols = slice(512 * c[0], 512 * c[1])
             nc.sync.dma_start(out=score.rearrange("(g m t) n -> g t m n", g=2, t=4)[b // 4, b % 4][:, cols], in_=q_of[b][:, cols])
 
-        s_grp = [kt("s_grp%d" % g, [P, R, 4], BF16) for g in range(2)]
+        s_grp = [work.tile([P, R, 4], BF16, name="sgrp%d" % g, tag="raw", bufs=2, align_bytes=64) for g in range(2)]
         s_codes = [kt("s_codes%d" % g, [P, R], U32) for g in range(2)]
         s_scales = [kt("s_scales%d" % g, [P, R], U8) for g in range(2)]
 
@@ -202,7 +208,7 @@ def tile_ligand_receptor_signalling_s8_kernel(
         n_scales = [kt("n_scales%d" % a, [P, 2 * P], U8) for a in range(4)]
 
         def n_widen(a, eng):
-            n_bf[a] = kt("n_bf%d" % a, [P, S], BF16)
+            n_bf[a] = work.tile([P, S], BF16, name="n_bf%d" % a, tag="lraw", bufs=8, align_bytes=64)
             copy(eng, n_bf[a][:], n_raw[:, a, :].bitcast(FP8))
 
         def n_T(a):
@@ -243,6 +249,7 @@ def tile_ligand_receptor_signalling_s8_kernel(
             "inter_piece": inter_piece, "inter_quant": inter_quant, "lig_T": lig_T, "lig_copy": lig_copy, "lig_quant": lig_quant,
             "h_mm1": h_mm1, "h_relu": h_relu, "ht_T": ht_T, "ht_copy": ht_copy, "ht_quant": ht_quant, "hs_piece": hs_piece, "hs_quant": hs_quant,
             "n_widen": n_widen, "n_T": n_T, "n_scale": n_scale, "n_quant": n_quant, "c_mm": c_mm, "c_copy": c_copy, "c_store": c_store,
+            "a_mm": a_mm, "hill_rsqrt": hill_rsqrt, "hill_square": hill_square, "hill_out": hill_out, "hill_store": hill_store,
         }
         engines = {"V": V, "S": SC, "G": nc.gpsimd}
 
@@ -251,54 +258,308 @@ def tile_ligand_receptor_signalling_s8_kernel(
                 calls[f[0]](*[engines.get(z, z) for z in f[1:]])
 
 
-        AFF=lambda b,n:'G'
-        RE=lambda b,h:'S' if (b,h) in((2,1),) else 'V'
-        NT={3:0,4:1,5:2,6:3}
-        hs=lambda g,k:('hs_piece',g,k,'V')
-        hq=lambda g,h:('hs_quant',g,h)
-        lc=lambda b:('lig_copy',b,'V'); lq=lambda b:('lig_quant',b)
-        ns=lambda a:('n_scale',a); nq=lambda a:('n_quant',a)
-        FILL={0:[[lc(4)],[],[lq(4)],[],[]],
-         1:[[lc(5)],[lq(5)],[hs(0,0)],[hs(0,1)],[]],
-         2:[[lc(6)],[lq(6)],[hs(0,2)],[hs(0,3)],[hq(0,0)]],
-         3:[[lc(7)],[lq(7)],[hq(0,1)],[],[ns(0)]],
-         4:[[nq(0),ns(1)],[],[],[nq(1)],[]],
-         5:[[ns(2)],[],[nq(2)],[],[]],
-         6:[[hs(1,0)],[hs(1,1),ns(3)],[],[],[nq(3),hs(1,2),hq(1,0),hs(1,3),hq(1,1)]],
-         7:[[],[],[],[],[]]}
-        LAST=[]
-        for a in range(4):
-            for h in range(2): LAST+=[('c_mm',a,h),('c_copy',a,h,'V'),('c_store',a,h)]
-
-
-        lig_T(0); lig_T(1)
-        inter_piece(0,0,0,V); inter_piece(0,0,1,SC); inter_piece(0,1,0,V); inter_piece(0,1,1,SC)
-        inter_quant(0,0); inter_piece(1,0,0,V); inter_piece(1,0,1,SC); inter_quant(0,1); inter_piece(1,1,0,V)
-        recip_kd(); lig_copy(0,SC); inter_quant(1,0); inter_piece(1,1,1,SC); lig_quant(0); lig_copy(1,SC); inter_quant(1,1)
-        h_mm1(0,0); h_relu(0,0,V); h_mm1(0,1); h_relu(0,1,SC); lig_quant(1)
-        n_widen(0,V)
-        h_mm1(1,0); h_relu(1,0,V); h_mm1(1,1);
-        ht_T(0); h_relu(1,1,SC); ht_copy(0,V)
-        lig_T(2); lig_copy(2,SC); n_widen(1,V); ht_quant(0); lig_quant(2); lig_T(3); lig_copy(3,SC); n_widen(2,V);  n_widen(3,V); lig_quant(3)
-        sq=[]
-        fill=FILL
-        for b in range(8):
-            for n in range(4):
-                a_mm(b,n)
-                sq.append((b,n))
-                if len(sq)>1:
-                    x,y=sq.pop(0); hill_square(x,(y,y+1)); hill_out(x,(y,y+1),engines[AFF(x,y)])
-                if n==1:
-                    if b<7: ht_T(b+1)
-                    if b<4: lig_T(b+4)
-                    if b in NT: n_T(NT[b])
-                    if b<7: ht_copy(b+1,V)
-                    run(fill[b][0])
-                    if b<7: ht_quant(b+1)
-                    run(fill[b][1])
-                if n>=2 and b<6:
-                    h_mm1(b+2,n-2); h_relu(b+2,n-2,engines[RE(b+2,n-2)])
-                    run(fill[b][n])
-            run(fill[b][4])
-        x,y=sq.pop(0); hill_square(x,(y,y+1)); hill_out(x,(y,y+1),engines[AFF(x,y)])
-        run(LAST)
+        inter_piece(0, 1, 0, engines["V"])
+        inter_piece(0, 0, 1, engines["S"])
+        inter_piece(0, 1, 1, engines["V"])
+        inter_piece(0, 0, 0, engines["V"])
+        inter_quant(0, 1)
+        inter_piece(1, 0, 1, engines["S"])
+        inter_piece(1, 0, 0, engines["V"])
+        inter_piece(1, 1, 1, engines["V"])
+        lig_T(1)
+        inter_piece(1, 1, 0, engines["S"])
+        inter_quant(1, 0)
+        lig_T(0)
+        inter_quant(0, 0)
+        lig_copy(1, engines["S"])
+        inter_quant(1, 1)
+        lig_copy(0, engines["S"])
+        lig_T(3)
+        lig_quant(1)
+        lig_quant(0)
+        h_mm1(1, 1)
+        lig_copy(3, engines["V"])
+        h_mm1(0, 0)
+        n_widen(0, engines["V"])
+        h_relu(1, 1, engines["S"])
+        h_mm1(0, 1)
+        lig_quant(3)
+        n_widen(1, engines["S"])
+        h_relu(0, 0, engines["V"])
+        lig_T(2)
+        h_relu(0, 1, engines["V"])
+        h_mm1(1, 0)
+        n_widen(2, engines["S"])
+        lig_copy(2, engines["V"])
+        ht_T(0)
+        n_widen(3, engines["V"])
+        h_mm1(3, 0)
+        ht_copy(0, engines["S"])
+        lig_quant(2)
+        h_mm1(2, 0)
+        h_relu(1, 0, engines["S"])
+        ht_quant(0)
+        a_mm(0, 2)
+        h_relu(3, 0, engines["S"])
+        h_relu(2, 0, engines["V"])
+        a_mm(0, 0)
+        recip_kd()
+        hill_rsqrt(0, 2)
+        hs_piece(0, 0, engines["V"])
+        a_mm(0, 1)
+        hs_piece(0, 1, engines["V"])
+        a_mm(0, 3)
+        hill_rsqrt(0, 1)
+        ht_T(1)
+        hill_square(0, (2, 3))
+        hs_quant(0, 0)
+        lig_T(4)
+        hill_rsqrt(0, 0)
+        ht_copy(1, engines["V"])
+        h_mm1(2, 1)
+        lig_copy(4, engines["S"])
+        hill_out(0, (2, 3), engines["V"])
+        h_mm1(3, 1)
+        ht_quant(1)
+        hill_store(0, (2, 3))
+        h_relu(2, 1, engines["S"])
+        lig_quant(4)
+        a_mm(1, 2)
+        h_relu(3, 1, engines["V"])
+        hill_square(0, (0, 1))
+        h_mm1(4, 0)
+        hill_rsqrt(1, 2)
+        hill_out(0, (0, 1), engines["V"])
+        h_mm1(4, 1)
+        hs_piece(0, 2, engines["V"])
+        hill_store(0, (0, 1))
+        hs_piece(0, 3, engines["S"])
+        a_mm(1, 1)
+        h_relu(4, 0, engines["V"])
+        ht_T(2)
+        h_relu(4, 1, engines["V"])
+        ht_T(3)
+        hill_rsqrt(0, 3)
+        a_mm(1, 0)
+        ht_copy(2, engines["V"])
+        ht_copy(3, engines["S"])
+        hs_quant(0, 1)
+        a_mm(1, 3)
+        hill_rsqrt(1, 0)
+        ht_quant(2)
+        ht_T(4)
+        ht_quant(3)
+        hill_rsqrt(1, 3)
+        lig_T(5)
+        ht_copy(4, engines["V"])
+        hill_square(0, (1, 2))
+        a_mm(3, 2)
+        lig_copy(5, engines["V"])
+        hill_rsqrt(1, 1)
+        a_mm(2, 1)
+        hill_out(0, (1, 2), engines["V"])
+        hill_rsqrt(3, 2)
+        ht_quant(4)
+        hill_store(0, (1, 2))
+        n_T(1)
+        lig_quant(5)
+        hill_square(0, (3, 4))
+        lig_T(7)
+        n_scale(1)
+        hill_square(1, (2, 3))
+        a_mm(2, 2)
+        hill_square(1, (0, 1))
+        a_mm(2, 3)
+        hill_out(0, (3, 4), engines["V"])
+        hill_rsqrt(2, 1)
+        hill_out(1, (0, 1), engines["V"])
+        hill_store(0, (3, 4))
+        h_mm1(5, 1)
+        lig_copy(7, engines["V"])
+        hill_square(3, (2, 3))
+        hill_store(1, (0, 1))
+        a_mm(3, 3)
+        hill_out(1, (2, 3), engines["V"])
+        hill_rsqrt(2, 3)
+        hill_out(3, (2, 3), engines["V"])
+        hill_store(1, (2, 3))
+        lig_quant(7)
+        hill_square(1, (1, 2))
+        a_mm(2, 0)
+        n_quant(1)
+        hill_store(3, (2, 3))
+        h_relu(5, 1, engines["V"])
+        hill_square(2, (1, 2))
+        n_T(0)
+        hill_out(1, (1, 2), engines["V"])
+        hill_square(1, (3, 4))
+        lig_T(6)
+        hill_out(2, (1, 2), engines["V"])
+        hill_store(1, (1, 2))
+        n_scale(0)
+        hill_rsqrt(2, 0)
+        h_mm1(7, 1)
+        hill_store(2, (1, 2))
+        hill_rsqrt(3, 3)
+        a_mm(3, 0)
+        lig_copy(6, engines["V"])
+        hill_rsqrt(2, 2)
+        h_mm1(5, 0)
+        hill_out(1, (3, 4), engines["V"])
+        hill_square(2, (3, 4))
+        lig_quant(6)
+        a_mm(4, 1)
+        hill_store(1, (3, 4))
+        h_relu(5, 0, engines["V"])
+        hill_rsqrt(3, 0)
+        a_mm(3, 1)
+        hill_out(2, (3, 4), engines["V"])
+        hill_square(2, (2, 3))
+        h_relu(7, 1, engines["V"])
+        a_mm(4, 3)
+        hill_store(2, (3, 4))
+        hill_square(3, (3, 4))
+        hill_out(2, (2, 3), engines["V"])
+        ht_T(5)
+        n_quant(0)
+        hill_store(2, (2, 3))
+        hill_rsqrt(4, 3)
+        h_mm1(6, 1)
+        hill_out(3, (3, 4), engines["V"])
+        ht_copy(5, engines["V"])
+        hill_store(3, (3, 4))
+        hill_square(3, (0, 1))
+        a_mm(4, 0)
+        h_relu(6, 1, engines["V"])
+        hill_rsqrt(4, 1)
+        h_mm1(6, 0)
+        ht_quant(5)
+        hill_rsqrt(3, 1)
+        hs_piece(1, 2, engines["V"])
+        a_mm(5, 1)
+        h_relu(6, 0, engines["S"])
+        hill_out(3, (0, 1), engines["V"])
+        n_T(3)
+        hs_piece(1, 3, engines["V"])
+        hill_store(3, (0, 1))
+        hill_square(2, (0, 1))
+        a_mm(4, 2)
+        n_scale(3)
+        hill_square(3, (1, 2))
+        h_mm1(7, 0)
+        hill_rsqrt(5, 1)
+        ht_T(6)
+        hill_out(3, (1, 2), engines["V"])
+        hill_square(4, (1, 2))
+        hill_out(2, (0, 1), engines["V"])
+        a_mm(5, 3)
+        hill_store(3, (1, 2))
+        ht_copy(6, engines["V"])
+        hill_rsqrt(4, 0)
+        hill_store(2, (0, 1))
+        n_T(2)
+        hill_out(4, (1, 2), engines["V"])
+        hill_rsqrt(5, 3)
+        hs_quant(1, 1)
+        hill_store(4, (1, 2))
+        a_mm(5, 0)
+        hill_rsqrt(4, 2)
+        n_quant(3)
+        ht_quant(6)
+        hill_square(4, (3, 4))
+        n_scale(2)
+        a_mm(6, 0)
+        h_relu(7, 0, engines["S"])
+        a_mm(6, 3)
+        hill_rsqrt(5, 0)
+        hill_out(4, (3, 4), engines["V"])
+        hs_piece(1, 0, engines["V"])
+        hill_rsqrt(6, 3)
+        hill_store(4, (3, 4))
+        a_mm(6, 2)
+        n_quant(2)
+        hill_square(5, (1, 2))
+        a_mm(6, 1)
+        hs_piece(1, 1, engines["V"])
+        hill_rsqrt(6, 0)
+        ht_T(7)
+        hill_out(5, (1, 2), engines["V"])
+        c_mm(2, 1)
+        hill_square(5, (0, 1))
+        hs_quant(1, 0)
+        hill_store(5, (1, 2))
+        hill_square(5, (3, 4))
+        a_mm(5, 2)
+        ht_copy(7, engines["V"])
+        hill_rsqrt(6, 1)
+        c_mm(2, 0)
+        hill_out(5, (0, 1), engines["V"])
+        hill_out(5, (3, 4), engines["V"])
+        hill_store(5, (0, 1))
+        hill_square(6, (0, 1))
+        c_mm(1, 0)
+        ht_quant(7)
+        c_copy(2, 1, engines["V"])
+        hill_store(5, (3, 4))
+        c_copy(2, 0, engines["S"])
+        a_mm(7, 0)
+        c_copy(1, 0, engines["V"])
+        hill_rsqrt(6, 2)
+        c_mm(0, 1)
+        c_store(2, 0)
+        c_store(2, 1)
+        hill_out(6, (0, 1), engines["V"])
+        c_mm(0, 0)
+        hill_square(6, (1, 2))
+        c_copy(0, 1, engines["V"])
+        c_mm(3, 0)
+        hill_rsqrt(5, 2)
+        hill_store(6, (0, 1))
+        hill_out(6, (1, 2), engines["V"])
+        c_copy(0, 0, engines["V"])
+        a_mm(7, 2)
+        hill_square(4, (0, 1))
+        hill_store(6, (1, 2))
+        c_copy(3, 0, engines["V"])
+        c_mm(3, 1)
+        c_store(0, 0)
+        c_store(0, 1)
+        hill_square(6, (2, 3))
+        hill_out(4, (0, 1), engines["V"])
+        c_mm(1, 1)
+        hill_rsqrt(7, 0)
+        hill_out(6, (2, 3), engines["V"])
+        c_copy(3, 1, engines["V"])
+        a_mm(7, 1)
+        hill_store(4, (0, 1))
+        hill_rsqrt(7, 2)
+        c_copy(1, 1, engines["V"])
+        a_mm(7, 3)
+        hill_store(6, (2, 3))
+        hill_square(6, (3, 4))
+        c_store(3, 0)
+        c_store(3, 1)
+        hill_rsqrt(7, 1)
+        hill_out(6, (3, 4), engines["V"])
+        hill_square(7, (0, 1))
+        hill_store(6, (3, 4))
+        hill_rsqrt(7, 3)
+        hill_out(7, (0, 1), engines["V"])
+        c_store(1, 0)
+        c_store(1, 1)
+        hill_square(4, (2, 3))
+        hill_square(7, (2, 3))
+        hill_out(4, (2, 3), engines["V"])
+        hill_store(7, (0, 1))
+        hill_square(5, (2, 3))
+        hill_out(7, (2, 3), engines["V"])
+        hill_store(4, (2, 3))
+        hill_square(7, (3, 4))
+        hill_out(5, (2, 3), engines["V"])
+        hill_store(7, (2, 3))
+        hill_square(7, (1, 2))
+        hill_out(7, (3, 4), engines["V"])
+        hill_store(5, (2, 3))
+        hill_out(7, (1, 2), engines["V"])
+        hill_store(7, (3, 4))
+        hill_store(7, (1, 2))

from contextlib import ExitStack

import concourse.mybir as mybir
from concourse.masks import make_identity

S, LIG, R, T, N = 1024, 1024, 1024, 2048, 512
FLOPS = 2 * (S * LIG * R + S * R * T + N * S * R)

P = 128
F32 = mybir.dt.float32
BF16 = mybir.dt.bfloat16
U32 = mybir.dt.uint32
I32 = mybir.dt.int32
U8 = mybir.dt.uint8
FP8 = mybir.dt.float8_e4m3fn
FP8X4 = mybir.dt.float8_e4m3fn_x4
FP4X4 = mybir.dt.float4_e2m1fn_x4
ACT = mybir.ActivationFunctionType
ALU = mybir.AluOpType


def tile_ligand_receptor_signalling_s8_kernel(
    tc, lig, inter, rec_words, rec_scales, niche_bytes, niche_scale, kd, score, contrast
):
    nc = tc.nc
    V, SC, TE = nc.vector, nc.scalar, nc.tensor

    with ExitStack() as ctx:
        keep = ctx.enter_context(tc.tile_pool(name="keep", bufs=1))
        work = ctx.enter_context(tc.tile_pool(name="work", bufs=3))
        psum = ctx.enter_context(tc.psum_pool(name="psum", bufs=1))
        ctx.enter_context(tc.manual_schedule())

        def kt(name, shape, dt):
            return keep.tile(shape, dt, name=name, align_bytes=64)

        kd_sb = kt("kd_sb", [P, 8], BF16)
        nsc = kt("nsc", [P, 8], F32)
        nc.scalar.dma_start(out=kd_sb[:].rearrange("p (g t) -> p g t", g=2), in_=kd.rearrange("(g m t) -> m g t", g=2, t=4))
        nc.scalar.dma_start(out=nsc[:].rearrange("p (g t) -> p g t", g=2), in_=niche_scale.rearrange("o (g p t) -> p (o g) t", g=2, t=4))

        rec_s = kt("rec_s", [P, 2, T], U8)
        nc.gpsimd.memset(rec_s[:].rearrange("p g n -> p (g n)").bitcast(I32), 0)
        ident = kt("ident", [P, P], F32)
        make_identity(nc, ident[:])

        i_raw = [work.tile([P, 4, R], BF16, name="raw%d" % g, tag="raw", bufs=2, align_bytes=64) for g in range(2)]
        inter_v = inter.rearrange("(g p j) r -> g p j r", g=2, j=4)
        l_raw = [work.tile([P, LIG], BF16, name="l_raw%d" % b, tag="lraw", bufs=8, align_bytes=64) for b in range(8)]
        lig_v = lig.rearrange("(g m t) k -> g m t k", g=2, t=4)
        rec_w = kt("rec_w", [P, 2, 2 * T], U8)
        n_raw = kt("n_raw", [P, 4, S], U8)

        def load_lig(b):
            nc.sync.dma_start(out=l_raw[b][:], in_=lig_v[b // 4, :, b % 4, :])

        def load_i(g):
            nc.sync.dma_start(out=i_raw[g][:], in_=inter_v[g])

        def load_n():
            nc.sync.dma_start(out=n_raw[:], in_=niche_bytes.rearrange("(a p) s -> p a s", p=P))

        def load_rs():
            for q in range(4):
                nc.sync.dma_start(
                    out=rec_s[32 * q : 32 * q + 4, :, :].bitcast(I32),
                    in_=rec_scales[:, 4 * q : 4 * q + 4, :].rearrange("g q n -> q g n").bitcast(I32),
                )

        def load_rw(g):
            nc.sync.dma_start(out=rec_w[:, g, :], in_=rec_words[g])

        loads = {"i": load_i, "l": load_lig, "n": load_n, "rs": load_rs, "rw": load_rw}
        LOADS=[('i',0),('i',1),('l',0),('l',1),('l',2),('l',3),('n',),('rs',),('rw',0),('rw',1),('l',4),('l',5),('l',6),('l',7)]
        for item in LOADS:
            loads[item[0]](*item[1:])

        warm = kt("warm", [P, 1], F32)
        nc.gpsimd.memset(warm[:], 1.0)
        SC.activation(out=warm[:], in_=warm[:], func=ACT.Abs_reciprocal_sqrt)

        def mx(out, a, asc, b, bsc, start, stop, bdt=FP8X4):
            TE.matmul_mx(out=out, lhsT=a.bitcast(FP8X4), lhsT_scale=asc, rhs=b.bitcast(bdt), rhs_scale=bsc, start=start, stop=stop)

        def quant(codes, scales, src):
            V.quantize_mx(out=codes.bitcast(FP8X4), scales=scales, in_=src)

        def copy(eng, out, in_):
            if eng is SC:
                SC.copy(out=out, in_=in_)
            else:
                V.tensor_copy(out=out, in_=in_)

        i_grp = [[kt("i_grp%d%d" % (g, h), [P, 2, P, 2, 4], BF16) for h in range(2)] for g in range(2)]
        i_codes = [kt("i_codes%d" % g, [P, R], U32) for g in range(2)]
        i_scales = [kt("i_scales%d" % g, [P, R], U8) for g in range(2)]

        def inter_piece(g, h, u, eng):
            src = i_raw[g][:, :, 512 * h : 512 * h + 512].rearrange("p j (q u e) -> p u q e j", u=2, e=2)
            copy(eng, i_grp[g][h][:, u], src[:, u])

        def inter_quant(g, h):
            cols = slice(512 * h, 512 * h + 512)
            quant(i_codes[g][:, cols], i_scales[g][:, cols], i_grp[g][h][:].rearrange("p u q e j -> p (u q e j)"))

        def word_transposes(words, step2):
            bank = psum.tile([P, 4, P], F32, name="tr", tag="tr", bufs=2)
            for c in range(4):
                if step2:
                    w = words[:, 256 * (c // 2) + c % 2 : 256 * (c // 2 + 1) : 2]
                else:
                    w = words[:, 128 * c : 128 * c + 128]
                TE.transpose(bank[:, c, :], w, ident[:])
            return bank

        l_grp = [None] * 8
        l_codes = [kt("l_codes%d" % b, [P, 2 * P], U32) for b in range(8)]
        l_scales = [kt("l_scales%d" % b, [P, 2 * P], U8) for b in range(8)]
        bank_of = {}

        def lig_T(b):
            bank_of["l", b] = word_transposes(l_raw[b][:].bitcast(F32), True)

        def lig_copy(b, eng):
            l_grp[b] = work.tile([P, 2, P, 4], BF16, name="l_grp", align_bytes=64)
            dst = l_grp[b][:].rearrange("p g m t -> p (g m t)").bitcast(F32).rearrange("p (g m u) -> p g m u", g=2, u=2)
            copy(eng, dst, bank_of["l", b][:].rearrange("p (g u) m -> p g m u", u=2))

        def lig_quant(b):
            quant(l_codes[b][:], l_scales[b][:], l_grp[b][:].rearrange("p g m t -> p (g m t)"))

        H = [kt("H%d" % g, [P, 4, R], BF16) for g in range(2)]

        def h_mm1(b, h):
                bank = psum.tile([P, 512], F32, name="hb", tag="hb", bufs=3)
                bank_of["h", b, h] = bank
                cols = slice(512 * h, 512 * h + 512)
                for g in range(2):
                    rows = slice(P * g, P * g + P)
                    mx(bank[:], l_codes[b][:, rows], l_scales[b][:, rows], i_codes[g][:, cols], i_scales[g][:, cols], g == 0, g == 1)

        def h_relu(b, h, eng):
            out = H[b // 4][:, b % 4, 512 * h : 512 * h + 512]
            if eng is SC:
                SC.activation(out=out, in_=bank_of["h", b, h][:], func=ACT.Relu)
            else:
                V.tensor_scalar(out=out, in0=bank_of["h", b, h][:], scalar1=0.0, scalar2=None, op0=ALU.max)

        t_grp = [None] * 8
        t_codes = [kt("t_codes%d" % b, [P, 2 * P], U32) for b in range(8)]
        t_scales = [kt("t_scales%d" % b, [P, 2 * P], U8) for b in range(8)]

        def ht_T(b):
            bank_of["t", b] = word_transposes(H[b // 4][:, b % 4, :].bitcast(F32), False)

        def ht_copy(b, eng):
            t_grp[b] = work.tile([P, 2, P, 4], BF16, name="t_grp", align_bytes=64)
            dst = t_grp[b][:].rearrange("p g m t -> p (g m t)").bitcast(F32).rearrange("p (g m u) -> p g m u", g=2, u=2)
            copy(eng, dst, bank_of["t", b][:].rearrange("p (g u) m -> p g m u", u=2))

        def ht_quant(b):
            quant(t_codes[b][:], t_scales[b][:], t_grp[b][:].rearrange("p g m t -> p (g m t)"))

        rkd = kt("rkd", [P, 8], F32)
        q_of = [None] * 8

        def a_mm(b, n):
            bank = psum.tile([P, 512], F32, name="ab", tag="ab", bufs=3)
            for g in range(2):
                rows = slice(P * g, P * g + P)
                mx(bank[:], t_codes[b][:, rows], t_scales[b][:, rows], rec_w[:, g, 1024 * n : 1024 * n + 1024],
                   rec_s[:, g, 512 * n : 512 * n + 512], g == 0, g == 1, FP4X4)
            bank_of["a", b, n] = bank

        def hill_rsqrt(b, n):
            if q_of[b] is None:
                q_of[b] = kt("q%d" % b, [P, T], F32)
            SC.activation(out=q_of[b][:, 512 * n : 512 * n + 512], in_=bank_of["a", b, n][:], func=ACT.Abs_reciprocal_sqrt,
                          scale=rkd[:, b : b + 1], bias=1.0)

        def hill_square(b, c):
            cols = slice(512 * c[0], 512 * c[1])
            SC.activation(out=q_of[b][:, cols], in_=q_of[b][:, cols], func=ACT.Square)

        def hill_out(b, c, eng):
            cols = slice(512 * c[0], 512 * c[1])
            eng.tensor_scalar(out=q_of[b][:, cols], in0=q_of[b][:, cols], scalar1=-1.0, scalar2=1.0, op0=ALU.mult, op1=ALU.add)

        def hill_store(b, c):
            cols = slice(512 * c[0], 512 * c[1])
            nc.sync.dma_start(out=score.rearrange("(g m t) n -> g t m n", g=2, t=4)[b // 4, b % 4][:, cols], in_=q_of[b][:, cols])

        s_grp = [work.tile([P, R, 4], BF16, name="sgrp%d" % g, tag="raw", bufs=2, align_bytes=64) for g in range(2)]
        s_codes = [kt("s_codes%d" % g, [P, R], U32) for g in range(2)]
        s_scales = [kt("s_scales%d" % g, [P, R], U8) for g in range(2)]

        def hs_piece(g, k, eng):
            cols = slice(256 * k, 256 * k + 256)
            copy(eng, s_grp[g][:, cols, :], H[g][:, :, cols].rearrange("p t r -> p r t"))

        def hs_quant(g, h):
            cols = slice(512 * h, 512 * h + 512)
            quant(s_codes[g][:, cols], s_scales[g][:, cols], s_grp[g][:, cols, :].rearrange("p r t -> p (r t)"))

        n_bf = [None] * 4
        n_grp = [None] * 4
        n_codes = [kt("n_codes%d" % a, [P, 2 * P], U32) for a in range(4)]
        n_scales = [kt("n_scales%d" % a, [P, 2 * P], U8) for a in range(4)]

        def n_widen(a, eng):
            n_bf[a] = work.tile([P, S], BF16, name="n_bf%d" % a, tag="lraw", bufs=8, align_bytes=64)
            copy(eng, n_bf[a][:], n_raw[:, a, :].bitcast(FP8))

        def n_T(a):
            bank_of["n", a] = word_transposes(n_bf[a][:].bitcast(F32), True)

        def n_scale(a):
            n_grp[a] = kt("n_grp%d" % a, [P, 2, P, 4], BF16)
            src = bank_of["n", a][:].rearrange("p c n -> p (c n)").bitcast(BF16).rearrange("p (g u n e) -> p g n u e", g=2, u=2, e=2)
            for g in range(2):
                sc = nsc[:, 4 * g : 4 * g + 4].rearrange("p (u e) -> p u e", e=2).unsqueeze(1).to_broadcast([P, P, 2, 2])
                V.tensor_tensor(out=n_grp[a][:, g].rearrange("p n (u e) -> p n u e", e=2), in0=src[:, g], in1=sc, op=ALU.mult)

        def n_quant(a):
            quant(n_codes[a][:], n_scales[a][:], n_grp[a][:].rearrange("p g n t -> p (g n t)"))

        c_out = [kt("c_out%d" % a, [P, R], F32) for a in range(4)]

        def c_mm(a, h):
            bank = psum.tile([P, 512], F32, name="hb", tag="hb", bufs=3)
            bank_of["c", a, h] = bank
            cols = slice(512 * h, 512 * h + 512)
            for g in range(2):
                rows = slice(P * g, P * g + P)
                mx(bank[:], n_codes[a][:, rows], n_scales[a][:, rows], s_codes[g][:, cols], s_scales[g][:, cols], g == 0, g == 1)

        def c_copy(a, h, eng):
            copy(eng, c_out[a][:, 512 * h : 512 * h + 512].rearrange("p (q u e) -> p q u e", u=2, e=2),
                 bank_of["c", a, h][:].rearrange("p (u q e) -> p q u e", u=2, e=2))

        def c_store(a, h):
            cols = slice(512 * h, 512 * h + 512)
            nc.sync.dma_start(out=contrast[P * a : P * a + P, cols], in_=c_out[a][:, cols])

        def recip_kd():
            V.reciprocal(out=rkd[:], in_=kd_sb[:])

        calls = {
            "inter_piece": inter_piece, "inter_quant": inter_quant, "lig_T": lig_T, "lig_copy": lig_copy, "lig_quant": lig_quant,
            "h_mm1": h_mm1, "h_relu": h_relu, "ht_T": ht_T, "ht_copy": ht_copy, "ht_quant": ht_quant, "hs_piece": hs_piece, "hs_quant": hs_quant,
            "n_widen": n_widen, "n_T": n_T, "n_scale": n_scale, "n_quant": n_quant, "c_mm": c_mm, "c_copy": c_copy, "c_store": c_store,
            "a_mm": a_mm, "hill_rsqrt": hill_rsqrt, "hill_square": hill_square, "hill_out": hill_out, "hill_store": hill_store,
        }
        engines = {"V": V, "S": SC, "G": nc.gpsimd}

        def run(items):
            for f in items:
                calls[f[0]](*[engines.get(z, z) for z in f[1:]])


        inter_piece(0, 1, 0, engines["V"])
        inter_piece(0, 0, 1, engines["S"])
        inter_piece(0, 1, 1, engines["V"])
        inter_piece(0, 0, 0, engines["V"])
        inter_quant(0, 1)
        inter_piece(1, 0, 1, engines["S"])
        inter_piece(1, 0, 0, engines["V"])
        inter_piece(1, 1, 1, engines["V"])
        lig_T(1)
        inter_piece(1, 1, 0, engines["S"])
        inter_quant(1, 0)
        lig_T(0)
        inter_quant(0, 0)
        lig_copy(1, engines["S"])
        inter_quant(1, 1)
        lig_copy(0, engines["S"])
        lig_T(3)
        lig_quant(1)
        lig_quant(0)
        h_mm1(1, 1)
        lig_copy(3, engines["V"])
        h_mm1(0, 0)
        n_widen(0, engines["V"])
        h_relu(1, 1, engines["S"])
        h_mm1(0, 1)
        lig_quant(3)
        n_widen(1, engines["S"])
        h_relu(0, 0, engines["V"])
        lig_T(2)
        h_relu(0, 1, engines["V"])
        h_mm1(1, 0)
        n_widen(2, engines["S"])
        lig_copy(2, engines["V"])
        ht_T(0)
        n_widen(3, engines["V"])
        h_mm1(3, 0)
        ht_copy(0, engines["S"])
        lig_quant(2)
        h_mm1(2, 0)
        h_relu(1, 0, engines["S"])
        ht_quant(0)
        a_mm(0, 2)
        h_relu(3, 0, engines["S"])
        h_relu(2, 0, engines["V"])
        a_mm(0, 0)
        recip_kd()
        hill_rsqrt(0, 2)
        hs_piece(0, 0, engines["V"])
        a_mm(0, 1)
        hs_piece(0, 1, engines["V"])
        a_mm(0, 3)
        hill_rsqrt(0, 1)
        ht_T(1)
        hill_square(0, (2, 3))
        hs_quant(0, 0)
        lig_T(4)
        hill_rsqrt(0, 0)
        ht_copy(1, engines["V"])
        h_mm1(2, 1)
        lig_copy(4, engines["S"])
        hill_out(0, (2, 3), engines["V"])
        h_mm1(3, 1)
        ht_quant(1)
        hill_store(0, (2, 3))
        h_relu(2, 1, engines["S"])
        lig_quant(4)
        a_mm(1, 2)
        h_relu(3, 1, engines["V"])
        hill_square(0, (0, 1))
        h_mm1(4, 0)
        hill_rsqrt(1, 2)
        hill_out(0, (0, 1), engines["V"])
        h_mm1(4, 1)
        hs_piece(0, 2, engines["V"])
        hill_store(0, (0, 1))
        hs_piece(0, 3, engines["S"])
        a_mm(1, 1)
        h_relu(4, 0, engines["V"])
        ht_T(2)
        h_relu(4, 1, engines["V"])
        ht_T(3)
        hill_rsqrt(0, 3)
        a_mm(1, 0)
        ht_copy(2, engines["V"])
        ht_copy(3, engines["S"])
        hs_quant(0, 1)
        a_mm(1, 3)
        hill_rsqrt(1, 0)
        ht_quant(2)
        ht_T(4)
        ht_quant(3)
        hill_rsqrt(1, 3)
        lig_T(5)
        ht_copy(4, engines["V"])
        hill_square(0, (1, 2))
        a_mm(3, 2)
        lig_copy(5, engines["V"])
        hill_rsqrt(1, 1)
        a_mm(2, 1)
        hill_out(0, (1, 2), engines["V"])
        hill_rsqrt(3, 2)
        ht_quant(4)
        hill_store(0, (1, 2))
        n_T(1)
        lig_quant(5)
        hill_square(0, (3, 4))
        lig_T(7)
        n_scale(1)
        hill_square(1, (2, 3))
        a_mm(2, 2)
        hill_square(1, (0, 1))
        a_mm(2, 3)
        hill_out(0, (3, 4), engines["V"])
        hill_rsqrt(2, 1)
        hill_out(1, (0, 1), engines["V"])
        hill_store(0, (3, 4))
        h_mm1(5, 1)
        lig_copy(7, engines["V"])
        hill_square(3, (2, 3))
        hill_store(1, (0, 1))
        a_mm(3, 3)
        hill_out(1, (2, 3), engines["V"])
        hill_rsqrt(2, 3)
        hill_out(3, (2, 3), engines["V"])
        hill_store(1, (2, 3))
        lig_quant(7)
        hill_square(1, (1, 2))
        a_mm(2, 0)
        n_quant(1)
        hill_store(3, (2, 3))
        h_relu(5, 1, engines["V"])
        hill_square(2, (1, 2))
        n_T(0)
        hill_out(1, (1, 2), engines["V"])
        hill_square(1, (3, 4))
        lig_T(6)
        hill_out(2, (1, 2), engines["V"])
        hill_store(1, (1, 2))
        n_scale(0)
        hill_rsqrt(2, 0)
        h_mm1(7, 1)
        hill_store(2, (1, 2))
        hill_rsqrt(3, 3)
        a_mm(3, 0)
        lig_copy(6, engines["V"])
        hill_rsqrt(2, 2)
        h_mm1(5, 0)
        hill_out(1, (3, 4), engines["V"])
        hill_square(2, (3, 4))
        lig_quant(6)
        a_mm(4, 1)
        hill_store(1, (3, 4))
        h_relu(5, 0, engines["V"])
        hill_rsqrt(3, 0)
        a_mm(3, 1)
        hill_out(2, (3, 4), engines["V"])
        hill_square(2, (2, 3))
        h_relu(7, 1, engines["V"])
        a_mm(4, 3)
        hill_store(2, (3, 4))
        hill_square(3, (3, 4))
        hill_out(2, (2, 3), engines["V"])
        ht_T(5)
        n_quant(0)
        hill_store(2, (2, 3))
        hill_rsqrt(4, 3)
        h_mm1(6, 1)
        hill_out(3, (3, 4), engines["V"])
        ht_copy(5, engines["V"])
        hill_store(3, (3, 4))
        hill_square(3, (0, 1))
        a_mm(4, 0)
        h_relu(6, 1, engines["V"])
        hill_rsqrt(4, 1)
        h_mm1(6, 0)
        ht_quant(5)
        hill_rsqrt(3, 1)
        hs_piece(1, 2, engines["V"])
        a_mm(5, 1)
        h_relu(6, 0, engines["S"])
        hill_out(3, (0, 1), engines["V"])
        n_T(3)
        hs_piece(1, 3, engines["V"])
        hill_store(3, (0, 1))
        hill_square(2, (0, 1))
        a_mm(4, 2)
        n_scale(3)
        hill_square(3, (1, 2))
        h_mm1(7, 0)
        hill_rsqrt(5, 1)
        ht_T(6)
        hill_out(3, (1, 2), engines["V"])
        hill_square(4, (1, 2))
        hill_out(2, (0, 1), engines["V"])
        a_mm(5, 3)
        hill_store(3, (1, 2))
        ht_copy(6, engines["V"])
        hill_rsqrt(4, 0)
        hill_store(2, (0, 1))
        n_T(2)
        hill_out(4, (1, 2), engines["V"])
        hill_rsqrt(5, 3)
        hs_quant(1, 1)
        hill_store(4, (1, 2))
        a_mm(5, 0)
        hill_rsqrt(4, 2)
        n_quant(3)
        ht_quant(6)
        hill_square(4, (3, 4))
        n_scale(2)
        a_mm(6, 0)
        h_relu(7, 0, engines["S"])
        a_mm(6, 3)
        hill_rsqrt(5, 0)
        hill_out(4, (3, 4), engines["V"])
        hs_piece(1, 0, engines["V"])
        hill_rsqrt(6, 3)
        hill_store(4, (3, 4))
        a_mm(6, 2)
        n_quant(2)
        hill_square(5, (1, 2))
        a_mm(6, 1)
        hs_piece(1, 1, engines["V"])
        hill_rsqrt(6, 0)
        ht_T(7)
        hill_out(5, (1, 2), engines["V"])
        c_mm(2, 1)
        hill_square(5, (0, 1))
        hs_quant(1, 0)
        hill_store(5, (1, 2))
        hill_square(5, (3, 4))
        a_mm(5, 2)
        ht_copy(7, engines["V"])
        hill_rsqrt(6, 1)
        c_mm(2, 0)
        hill_out(5, (0, 1), engines["V"])
        hill_out(5, (3, 4), engines["V"])
        hill_store(5, (0, 1))
        hill_square(6, (0, 1))
        c_mm(1, 0)
        ht_quant(7)
        c_copy(2, 1, engines["V"])
        hill_store(5, (3, 4))
        c_copy(2, 0, engines["S"])
        a_mm(7, 0)
        c_copy(1, 0, engines["V"])
        hill_rsqrt(6, 2)
        c_mm(0, 1)
        c_store(2, 0)
        c_store(2, 1)
        hill_out(6, (0, 1), engines["V"])
        c_mm(0, 0)
        hill_square(6, (1, 2))
        c_copy(0, 1, engines["V"])
        c_mm(3, 0)
        hill_rsqrt(5, 2)
        hill_store(6, (0, 1))
        hill_out(6, (1, 2), engines["V"])
        c_copy(0, 0, engines["V"])
        a_mm(7, 2)
        hill_square(4, (0, 1))
        hill_store(6, (1, 2))
        c_copy(3, 0, engines["V"])
        c_mm(3, 1)
        c_store(0, 0)
        c_store(0, 1)
        hill_square(6, (2, 3))
        hill_out(4, (0, 1), engines["V"])
        c_mm(1, 1)
        hill_rsqrt(7, 0)
        hill_out(6, (2, 3), engines["V"])
        c_copy(3, 1, engines["V"])
        a_mm(7, 1)
        hill_store(4, (0, 1))
        hill_rsqrt(7, 2)
        c_copy(1, 1, engines["V"])
        a_mm(7, 3)
        hill_store(6, (2, 3))
        hill_square(6, (3, 4))
        c_store(3, 0)
        c_store(3, 1)
        hill_rsqrt(7, 1)
        hill_out(6, (3, 4), engines["V"])
        hill_square(7, (0, 1))
        hill_store(6, (3, 4))
        hill_rsqrt(7, 3)
        hill_out(7, (0, 1), engines["V"])
        c_store(1, 0)
        c_store(1, 1)
        hill_square(4, (2, 3))
        hill_square(7, (2, 3))
        hill_out(4, (2, 3), engines["V"])
        hill_store(7, (0, 1))
        hill_square(5, (2, 3))
        hill_out(7, (2, 3), engines["V"])
        hill_store(4, (2, 3))
        hill_square(7, (3, 4))
        hill_out(5, (2, 3), engines["V"])
        hill_store(7, (2, 3))
        hill_square(7, (1, 2))
        hill_out(7, (3, 4), engines["V"])
        hill_store(5, (2, 3))
        hill_out(7, (1, 2), engines["V"])
        hill_store(7, (3, 4))
        hill_store(7, (1, 2))
